import numpy as np, ml_dtypes
CORES = [136,8,152,24,168,40,184,56,200,72,216,88,232,104,248,120]
N = 16
TK = 256
def setup_inputs(rng):
    return {"x": rng.standard_normal((N, 128, TK), dtype=np.float32).astype(ml_dtypes.bfloat16), "w": rng.standard_normal((N, 128, N * 128), dtype=np.float32).astype(ml_dtypes.bfloat16)}
def reference(x, w):
    X, W = x.astype(np.float64), w.astype(np.float64)
    y = np.zeros((N, 128, TK))
    for r in range(N):
        for j in range(N):
            y[r] += W[r][:, 128 * j:128 * j + 128].T @ X[j]
    return {"y": y.astype(ml_dtypes.bfloat16 if x.dtype != np.float64 else np.float64)}

@@ -1,0 +1,135 @@
+from concourse.bass import DstId, RemoteDMATransfer
+
+N = 16
+TK = 256
+P = 128
+
+DIRECT = 3
+QUOTA_OWN_DIE = 8
+HELP_SAME = 3
+HELP_OTHER = 4
+WCH = 2
+
+SCRATCH = {
+    "xd": ("dram", [P, TK], "bfloat16"),
+    "xg": ("sbuf", [P, N * TK], "bfloat16"),
+    "ws": ("sbuf", [P, N * P], "bfloat16"),
+    "ys": ("sbuf", [P, TK], "bfloat16"),
+    "ps": ("psum", [P, TK], "float32"),
+}
+SEMAPHORES = (["xl", "xs", "got", "sent", "mm", "cp", "st"] + ["w%d" % k for k in range(WCH)]
+              + ["a%d" % j for j in range(N)])
+
+
+def _bits(m):
+    return bin(m).count("1")
+
+
+def _chip_cores(core, topo):
+    n = topo.CORES_PER_CHIP
+    base = core - core % n
+    return [c for c in range(base, base + n) if topo.host(c) == topo.host(core) and topo.chip(c) == topo.chip(core)]
+
+
+def _plan(owner, chipc, topo):
+    same = [c for c in chipc if c != owner and topo.die(c) == topo.die(owner)][:HELP_SAME]
+    other = [c for c in chipc if topo.die(c) != topo.die(owner)][:HELP_OTHER]
+    cnt = {}
+    for grp, quota in ((other, N - 1 - QUOTA_OWN_DIE), (same, QUOTA_OWN_DIE - DIRECT)):
+        for i, c in enumerate(grp):
+            cnt[c] = quota // len(grp) + (1 if i < quota % len(grp) else 0)
+    turns = []
+    for i in range(max(len(same), len(other))):
+        if i < len(other):
+            turns.append(other[i])
+        if i < len(same):
+            turns.append(same[i])
+    order = sorted([c for c in turns if cnt[c] > 0], key=lambda c: -cnt[c])
+    offs = {c: [] for c in order}
+    nxt = 1 + DIRECT
+    wave = 0
+    while nxt < N:
+        for c in order:
+            if cnt[c] > wave:
+                offs[c].append(nxt)
+                nxt += 1
+        wave += 1
+    return list(range(1, 1 + DIRECT)), [(c, offs[c]) for c in order]
+
+
+def _send(g, core, T, topo, me, offs):
+    dests = [T.cores[(me + d) % N] for d in offs]
+    m = topo.mask(core, dests[0])
+    for c in dests:
+        m &= topo.mask(core, c)
+    ids = []
+    for c in dests:
+        rid, pid = topo.addr(c, core)
+        ids.append(DstId(rid=rid, pnc=pid))
+    tr = RemoteDMATransfer(dst_ids=ids, dma_engine_mask=m, remote_sem=T.sem["a%d" % me], srcs=[T.xd[:, :]],
+                           dsts=[T.xg[:, me * TK:(me + 1) * TK] for _ in dests])
+    g.remote_dma_fused([tr], local_sem=T.sem.sent)
+    return _bits(m)
+
+
+def rank_program(g, core, T, topo):
+    chipc = _chip_cores(core, topo)
+    owners = [c for c in chipc if T.rank_of(c) is not None]
+    if not owners:
+        return
+    owner = owners[0]
+    me = T.rank_of(owner)
+    own_offs, helpers = _plan(owner, chipc, topo)
+
+    if core != owner:
+        mine = [o for c, o in helpers if c == core]
+        if not mine:
+            return
+        g.wait_ge(T.sem.got, _bits(topo.mask(owner, core)))
+        n = _send(g, core, T, topo, me, mine[0])
+        g.wait_ge(T.sem.sent, n)
+        return
+
+    g.sync.dma_start(T.xd[:, :], T.x[:, :]).then_inc(T.sem.xl, 16)
+    g.scalar.dma_start(T.xg[:, me * TK:(me + 1) * TK], T.x[:, :]).then_inc(T.sem.xs, 16)
+    wc = N * P // WCH
+    first = (me * P) // wc
+    for i in range(WCH):
+        k = (first - i) % WCH
+        q = g.scalar if i % 2 == 0 else g.sync
+        q.dma_start(T.ws[:, k * wc:(k + 1) * wc], T.w[:, k * wc:(k + 1) * wc]).then_inc(T.sem["w%d" % k], 16)
+
+    g.wait_ge(T.sem.xl, 16)
+    hm = topo.mask(owner, helpers[0][0])
+    ids = []
+    for c, _o in helpers:
+        hm &= topo.mask(owner, c)
+        rid, pid = topo.addr(c, owner)
+        ids.append(DstId(rid=rid, pnc=pid))
+    tr = RemoteDMATransfer(dst_ids=ids, dma_engine_mask=hm, remote_sem=T.sem.got, srcs=[T.xd[:, :]],
+                           dsts=[T.xd[:, :] for _ in helpers])
+    g.remote_dma_fused([tr], local_sem=T.sem.sent)
+    left = _bits(hm)
+    left += _send(g, core, T, topo, me, own_offs)
+
+    waited = []
+    mm = None
+    for d in range(N):
+        j = (me - d) % N
+        k = (j * P) // wc
+        if k not in waited:
+            g.tensor.wait_ge(T.sem["w%d" % k], 16)
+            waited.append(k)
+        if d == 0:
+            g.tensor.wait_ge(T.sem.xs, 16)
+        else:
+            g.tensor.wait_ge(T.sem["a%d" % j], _bits(topo.mask(T.cores[j], core)))
+        mm = g.tensor.matmul(T.ps[:, :], T.ws[:, j * P:(j + 1) * P], T.xg[:, j * TK:(j + 1) * TK], d == 0, d == N - 1)
+    mm.then_inc(T.sem.mm, 1)
+
+    g.vector.wait_ge(T.sem.mm, 1)
+    g.vector.tensor_copy(T.ys[:, :], T.ps[:, :]).then_inc(T.sem.cp, 1)
+    g.sync.wait_ge(T.sem.cp, 1)
+    g.sync.dma_start(T.y[:, :], T.ys[:, :]).then_inc(T.sem.st, 16)
+    g.sync.wait_ge(T.sem.st, 16)
+    g.wait_ge(T.sem.sent, left)

@@ -4,9 +4,9 @@ N = 16
 TK = 256
 P = 128
 
-DIRECT = 3
+DIRECT = 6
 QUOTA_OWN_DIE = 8
-HELP_SAME = 3
+HELP_SAME = 1
 HELP_OTHER = 4
 WCH = 2
 
@@ -57,19 +57,17 @@ def _plan(owner, chipc, topo):
     return list(range(1, 1 + DIRECT)), [(c, offs[c]) for c in order]
 
 
-def _send(g, core, T, topo, me, offs):
+def _away(core, T, topo, me, offs):
     dests = [T.cores[(me + d) % N] for d in offs]
     m = topo.mask(core, dests[0])
-    for c in dests:
-        m &= topo.mask(core, c)
     ids = []
     for c in dests:
+        m &= topo.mask(core, c)
         rid, pid = topo.addr(c, core)
         ids.append(DstId(rid=rid, pnc=pid))
     tr = RemoteDMATransfer(dst_ids=ids, dma_engine_mask=m, remote_sem=T.sem["a%d" % me], srcs=[T.xd[:, :]],
                            dsts=[T.xg[:, me * TK:(me + 1) * TK] for _ in dests])
-    g.remote_dma_fused([tr], local_sem=T.sem.sent)
-    return _bits(m)
+    return tr, m
 
 
 def rank_program(g, core, T, topo):
@@ -81,13 +79,20 @@ def rank_program(g, core, T, topo):
     me = T.rank_of(owner)
     own_offs, helpers = _plan(owner, chipc, topo)
 
+    direct, dm = _away(owner, T, topo, me, own_offs)
+    hm = topo.mask(owner, helpers[0][0])
+    for c, _o in helpers:
+        hm &= topo.mask(owner, c)
+    hm &= ~dm
+
     if core != owner:
         mine = [o for c, o in helpers if c == core]
         if not mine:
             return
-        g.wait_ge(T.sem.got, _bits(topo.mask(owner, core)))
-        n = _send(g, core, T, topo, me, mine[0])
-        g.wait_ge(T.sem.sent, n)
+        g.wait_ge(T.sem.got, _bits(hm))
+        tr, m = _away(core, T, topo, me, mine[0])
+        g.remote_dma_fused([tr], local_sem=T.sem.sent)
+        g.wait_ge(T.sem.sent, _bits(m))
         return
 
     g.sync.dma_start(T.xd[:, :], T.x[:, :]).then_inc(T.sem.xl, 16)
@@ -100,17 +105,13 @@ def rank_program(g, core, T, topo):
         q.dma_start(T.ws[:, k * wc:(k + 1) * wc], T.w[:, k * wc:(k + 1) * wc]).then_inc(T.sem["w%d" % k], 16)
 
     g.wait_ge(T.sem.xl, 16)
-    hm = topo.mask(owner, helpers[0][0])
     ids = []
     for c, _o in helpers:
-        hm &= topo.mask(owner, c)
         rid, pid = topo.addr(c, owner)
         ids.append(DstId(rid=rid, pnc=pid))
-    tr = RemoteDMATransfer(dst_ids=ids, dma_engine_mask=hm, remote_sem=T.sem.got, srcs=[T.xd[:, :]],
-                           dsts=[T.xd[:, :] for _ in helpers])
-    g.remote_dma_fused([tr], local_sem=T.sem.sent)
-    left = _bits(hm)
-    left += _send(g, core, T, topo, me, own_offs)
+    hand = RemoteDMATransfer(dst_ids=ids, dma_engine_mask=hm, remote_sem=T.sem.got, srcs=[T.xd[:, :]],
+                             dsts=[T.xd[:, :] for _ in helpers])
+    g.remote_dma_fused([hand, direct], local_sem=T.sem.sent)
 
     waited = []
     mm = None
@@ -132,4 +133,4 @@ def rank_program(g, core, T, topo):
     g.sync.wait_ge(T.sem.cp, 1)
     g.sync.dma_start(T.y[:, :], T.ys[:, :]).then_inc(T.sem.st, 16)
     g.sync.wait_ge(T.sem.st, 16)
-    g.wait_ge(T.sem.sent, left)
+    g.wait_ge(T.sem.sent, _bits(hm) + _bits(dm))

from concourse.bass import DstId, RemoteDMATransfer

N = 16
TK = 256
P = 128

DIRECT = 6
QUOTA_OWN_DIE = 8
HELP_SAME = 1
HELP_OTHER = 4
WCH = 2

SCRATCH = {
    "xd": ("dram", [P, TK], "bfloat16"),
    "xg": ("sbuf", [P, N * TK], "bfloat16"),
    "ws": ("sbuf", [P, N * P], "bfloat16"),
    "ys": ("sbuf", [P, TK], "bfloat16"),
    "ps": ("psum", [P, TK], "float32"),
}
SEMAPHORES = (["xl", "xs", "got", "sent", "mm", "cp", "st"] + ["w%d" % k for k in range(WCH)]
              + ["a%d" % j for j in range(N)])


def _bits(m):
    return bin(m).count("1")


def _chip_cores(core, topo):
    n = topo.CORES_PER_CHIP
    base = core - core % n
    return [c for c in range(base, base + n) if topo.host(c) == topo.host(core) and topo.chip(c) == topo.chip(core)]


def _plan(owner, chipc, topo):
    same = [c for c in chipc if c != owner and topo.die(c) == topo.die(owner)][:HELP_SAME]
    other = [c for c in chipc if topo.die(c) != topo.die(owner)][:HELP_OTHER]
    cnt = {}
    for grp, quota in ((other, N - 1 - QUOTA_OWN_DIE), (same, QUOTA_OWN_DIE - DIRECT)):
        for i, c in enumerate(grp):
            cnt[c] = quota // len(grp) + (1 if i < quota % len(grp) else 0)
    turns = []
    for i in range(max(len(same), len(other))):
        if i < len(other):
            turns.append(other[i])
        if i < len(same):
            turns.append(same[i])
    order = sorted([c for c in turns if cnt[c] > 0], key=lambda c: -cnt[c])
    offs = {c: [] for c in order}
    nxt = 1 + DIRECT
    wave = 0
    while nxt < N:
        for c in order:
            if cnt[c] > wave:
                offs[c].append(nxt)
                nxt += 1
        wave += 1
    return list(range(1, 1 + DIRECT)), [(c, offs[c]) for c in order]


def _away(core, T, topo, me, offs):
    dests = [T.cores[(me + d) % N] for d in offs]
    m = topo.mask(core, dests[0])
    ids = []
    for c in dests:
        m &= topo.mask(core, c)
        rid, pid = topo.addr(c, core)
        ids.append(DstId(rid=rid, pnc=pid))
    tr = RemoteDMATransfer(dst_ids=ids, dma_engine_mask=m, remote_sem=T.sem["a%d" % me], srcs=[T.xd[:, :]],
                           dsts=[T.xg[:, me * TK:(me + 1) * TK] for _ in dests])
    return tr, m


def rank_program(g, core, T, topo):
    chipc = _chip_cores(core, topo)
    owners = [c for c in chipc if T.rank_of(c) is not None]
    if not owners:
        return
    owner = owners[0]
    me = T.rank_of(owner)
    own_offs, helpers = _plan(owner, chipc, topo)

    direct, dm = _away(owner, T, topo, me, own_offs)
    hm = topo.mask(owner, helpers[0][0])
    for c, _o in helpers:
        hm &= topo.mask(owner, c)
    hm &= ~dm

    if core != owner:
        mine = [o for c, o in helpers if c == core]
        if not mine:
            return
        g.wait_ge(T.sem.got, _bits(hm))
        tr, m = _away(core, T, topo, me, mine[0])
        g.remote_dma_fused([tr], local_sem=T.sem.sent)
        g.wait_ge(T.sem.sent, _bits(m))
        return

    g.sync.dma_start(T.xd[:, :], T.x[:, :]).then_inc(T.sem.xl, 16)
    g.scalar.dma_start(T.xg[:, me * TK:(me + 1) * TK], T.x[:, :]).then_inc(T.sem.xs, 16)
    wc = N * P // WCH
    first = (me * P) // wc
    for i in range(WCH):
        k = (first - i) % WCH
        q = g.scalar if i % 2 == 0 else g.sync
        q.dma_start(T.ws[:, k * wc:(k + 1) * wc], T.w[:, k * wc:(k + 1) * wc]).then_inc(T.sem["w%d" % k], 16)

    g.wait_ge(T.sem.xl, 16)
    ids = []
    for c, _o in helpers:
        rid, pid = topo.addr(c, owner)
        ids.append(DstId(rid=rid, pnc=pid))
    hand = RemoteDMATransfer(dst_ids=ids, dma_engine_mask=hm, remote_sem=T.sem.got, srcs=[T.xd[:, :]],
                             dsts=[T.xd[:, :] for _ in helpers])
    g.remote_dma_fused([hand, direct], local_sem=T.sem.sent)

    waited = []
    mm = None
    for d in range(N):
        j = (me - d) % N
        k = (j * P) // wc
        if k not in waited:
            g.tensor.wait_ge(T.sem["w%d" % k], 16)
            waited.append(k)
        if d == 0:
            g.tensor.wait_ge(T.sem.xs, 16)
        else:
            g.tensor.wait_ge(T.sem["a%d" % j], _bits(topo.mask(T.cores[j], core)))
        mm = g.tensor.matmul(T.ps[:, :], T.ws[:, j * P:(j + 1) * P], T.xg[:, j * TK:(j + 1) * TK], d == 0, d == N - 1)
    mm.then_inc(T.sem.mm, 1)

    g.vector.wait_ge(T.sem.mm, 1)
    g.vector.tensor_copy(T.ys[:, :], T.ps[:, :]).then_inc(T.sem.cp, 1)
    g.sync.wait_ge(T.sem.cp, 1)
    g.sync.dma_start(T.y[:, :], T.ys[:, :]).then_inc(T.sem.st, 16)
    g.sync.wait_ge(T.sem.st, 16)
    g.wait_ge(T.sem.sent, _bits(hm) + _bits(dm))
